import numpy as np
import ml_dtypes


def mxq(x, axis, fmt="e4m3"):
    dtype, down = {"e4m3": (ml_dtypes.float8_e4m3fn, 7), "e5m2": (ml_dtypes.float8_e5m2, 14)}[fmt]
    v = np.moveaxis(np.asarray(x, np.float32).astype(ml_dtypes.bfloat16).astype(np.float64), axis, -1)
    blocks = v.reshape(v.shape[:-1] + (-1, 32))
    amax = np.abs(blocks).max(-1, keepdims=True)
    byte = np.maximum(np.where(amax > 0, np.frexp(amax)[1] - 1 + 127, 0) - down, 1)
    scale = np.exp2(byte - 127.0)
    codes = (blocks / scale).astype(np.float32).astype(dtype).astype(np.float64)
    return np.moveaxis((codes * scale).reshape(v.shape), -1, axis)


WIDE = False


def mx_kscale(k):
    if not WIDE:
        return np.ones(k)
    levels = np.array([10, -10, 5, -5, 0])
    if k % 512:
        return np.exp2(np.random.permutation(np.resize(levels, k // 32))).repeat(32)
    a = np.empty((k // 512, 16))
    for p in range(k // 512):
        a[p, :8] = np.random.permutation(np.resize(levels, 8))
        for g in range(8):
            far = levels[np.abs(levels - a[p, g]) >= 10]
            a[p, g + 8] = far[np.random.randint(len(far))]
    return np.exp2(a.ravel()).repeat(32)


def f64(x):
    return np.asarray(x).astype(np.float64)


def striped(idx):
    return np.tile(idx.reshape(-1, 16).T, (8, 1)).astype(np.uint16)


def unstriped(offs):
    return offs[:16].T.reshape(-1).astype(np.int64)


def striped8(idx):
    return np.concatenate([x.reshape(-1, 16).T for x in idx]).astype(np.uint16)


def runs(offs, k):
    lists = np.stack([offs[16 * r : 16 * r + 16].T.reshape(-1) for r in range(8)]).astype(np.int64)
    return lists[np.arange(k) % 512 // 64]


def pack_weight(w):
    k, n = w.shape
    w = f64(np.asarray(w, np.float32).astype(ml_dtypes.bfloat16)).reshape(k // 32, 32, n)
    amax = np.abs(w).max(1)
    byte = np.clip(np.where(amax > 0, np.frexp(amax)[1] - 1 + 127 - 7, 1), 1, 254)
    scaled = (w * np.exp2(127.0 - byte)[:, None, :]).reshape(k, n).astype(np.float32)
    words = np.ascontiguousarray(scaled.reshape(k // 512, 128, 4, n).transpose(0, 1, 3, 2)).astype(ml_dtypes.float8_e4m3fn).view(np.uint8)
    return words, np.ascontiguousarray(byte.astype(np.uint8).reshape(k // 512, 16, n))


def unpack_weight(words, scales):
    g, p, n, _ = words.shape
    vals = np.ascontiguousarray(words).view(ml_dtypes.float8_e4m3fn).astype(np.float64) * np.repeat(np.exp2(scales.astype(np.float64) - 127.0), 8, axis=1)[..., None]
    return vals.transpose(0, 1, 3, 2).reshape(g * 512, n)

def planes(y):
    n, m = y.shape
    v = y.astype(np.float32).astype(ml_dtypes.bfloat16).astype(np.float64).reshape(n // 32, 32, m)
    top = np.abs(v).max(1)
    byte = np.clip(np.where(top > 0, np.frexp(top)[1] - 1 + 127 - 7, 1), 1, 254)
    codes = (v * np.exp2(127.0 - byte)[:, None, :]).reshape(n, m).astype(np.float32).astype(ml_dtypes.float8_e4m3fn).view(np.uint8)
    words = codes.reshape(n // 512, 128, 4, m).transpose(0, 1, 3, 2)
    return np.ascontiguousarray(words), np.ascontiguousarray(byte.astype(np.uint8).reshape(n // 512, 16, m))


K, T, S, H, G = 512, 2048, 512, 512, 2048


def setup_inputs():
    n = np.random.standard_normal
    s = mx_kscale(K)[:, None]
    packed_xT = pack_weight(n((K, T)) * s)
    packed_w1 = pack_weight(n((K, H)) / np.sqrt(K) / s)
    packed_dT = pack_weight(n((K, G)) / s)
    return {
        "x_words": packed_xT[0],
        "x_scales": packed_xT[1],
        "w1_words": packed_w1[0],
        "w1_scales": packed_w1[1],
        "gs": (np.random.uniform(0.5, 1.5, (K, 1)) * s).astype(np.float32),
        "d_words": packed_dT[0],
        "d_scales": packed_dT[1],
        "offs": striped(np.random.permutation(T)[:S]),
        "n1": striped8(np.stack([np.random.permutation(S) for _ in range(8)])),
        "n2": striped8(np.stack([np.random.permutation(S) for _ in range(8)])),
        "k1": striped8(np.random.randint(0, G, (8, H))),
        "n3": striped8(np.stack([np.random.permutation(S) for _ in range(8)])),
    }


def reference(x_words, x_scales, w1_words, w1_scales, gs, d_words, d_scales, offs, n1, n2, k1, n3):
    d_k1 = unpack_weight(d_words, d_scales)[np.arange(K)[:, None], runs(k1, K)]
    xq = unpack_weight(x_words, x_scales)[:, unstriped(offs)]
    y = unpack_weight(w1_words, w1_scales).T @ xq
    z = f64(gs) * ((y[np.arange(H)[:, None], runs(n1, H)]) * (y[np.arange(H)[:, None], runs(n2, H)]))
    h = 0.0625 * ((d_k1.T @ mxq(z, 0, "e4m3")))
    pa = h[np.arange(H)[:, None], runs(n3, H)]
    out_0 = (2.0 * (h * pa)) / ((h) ** 2 + (pa) ** 2 + 0.5)
    return (out_0,) + planes(out_0)

@@ -1,0 +1,237 @@
+from contextlib import ExitStack
+
+import concourse.mybir as mybir
+
+F32 = mybir.dt.float32
+BF16 = mybir.dt.bfloat16
+I32 = mybir.dt.int32
+U32 = mybir.dt.uint32
+U16 = mybir.dt.uint16
+U8 = mybir.dt.uint8
+FP8X4 = mybir.dt.float8_e4m3fn_x4
+ACT = mybir.ActivationFunctionType
+MULT = mybir.AluOpType.mult
+ADD = mybir.AluOpType.add
+
+P = 128
+PACK = 4
+S = 512
+TABLE = 2048
+CH = 128
+NCH = S // CH
+Z_PIECES = ((0, 256), (256, 384), (384, 512))
+FLOPS = 2 * 2 * 512 * 512 * 512
+
+
+def deal(engine, dst, src, run):
+    engine.tensor_copy(
+        out=dst.rearrange("p (t b i) -> p b t i", t=PACK, i=run),
+        in_=src.rearrange("p (b i t) -> p b t i", t=PACK, i=run),
+    )
+
+
+def interleave(nc, dst, src):
+    nc.scalar.copy(
+        out=dst.rearrange("p (c i t) -> p c t i", t=PACK, i=PACK),
+        in_=src.rearrange("p t (c i) -> p c t i", i=PACK),
+    )
+
+
+def tile_picked_denseprodharm_none_po_kernel(
+    tc, x_words, x_scales, w1_words, w1_scales, gs, d_words, d_scales, offs, n1, n2, k1, n3, out_0, out_1, out_2
+):
+    nc = tc.nc
+    with ExitStack() as ctx:
+        sb = ctx.enter_context(tc.tile_pool(name="sb", bufs=1))
+        ps = ctx.enter_context(tc.psum_pool(name="ps", bufs=1))
+
+        def tile(name, shape, dtype, slot=None):
+            return sb.tile(shape, dtype, name=name, tag=slot or name, align_bytes=64)
+
+        lists = {}
+        for name in ("offs", "n1", "n2", "k1", "n3"):
+            lists[name] = tile("list_" + name, [P, S // 16], U16)
+
+        def entries(name, lo, hi):
+            return lists[name][:, lo // 16 : hi // 16]
+
+        def words_of(ap):
+            return ap[0].rearrange("p n t -> p (n t)").bitcast(I32)
+
+        xs_win = tile("xs_win", [P, TABLE], U8)
+        w1s_raw = tile("w1s_raw", [P, S], U8)
+        ds_win = tile("ds_win", [P, TABLE], U8)
+        ds_plane = tile("ds_plane", [P, S], U8)
+        warm = tile("warm", [P, 2], F32)
+        nc.vector.memset(xs_win[:].bitcast(I32), 0)
+        nc.vector.memset(w1s_raw[:].bitcast(I32), 0)
+        nc.vector.memset(warm[:, 0:1], 1.0)
+        nc.vector.memset(ds_win[:].bitcast(I32), 0)
+        nc.vector.memset(ds_plane[:].bitcast(I32), 0)
+
+        xw_win = tile("xw_win", [P, TABLE], I32)
+        w1w_raw = tile("w1w_raw", [P, S], I32)
+        dw_win = tile("dw_win", [P, TABLE], I32)
+        gain = tile("gain", [P, PACK], F32)
+
+        nc.sync.dma_start(lists["offs"][:], offs)
+        nc.sync.dma_start(lists["k1"][:], k1)
+        nc.sync.dma_start(lists["n1"][:], n1)
+        nc.sync.dma_start(xw_win[:], words_of(x_words))
+        nc.gpsimd.dma_start(gain[:], gs.rearrange("(p t) o -> p (t o)", t=PACK))
+        for q in range(4):
+            nc.scalar.dma_start(xs_win[32 * q : 32 * q + 4, :].bitcast(I32), x_scales[0, 4 * q : 4 * q + 4, :].bitcast(I32))
+        nc.scalar.activation(warm[:, 1:2], warm[:, 0:1], ACT.Abs_reciprocal_sqrt)
+        nc.sync.dma_start(w1w_raw[:], words_of(w1_words))
+        for q in range(4):
+            nc.scalar.dma_start(w1s_raw[32 * q : 32 * q + 4, :].bitcast(I32), w1_scales[0, 4 * q : 4 * q + 4, :].bitcast(I32))
+        nc.sync.dma_start(ds_win[0:P:8, :].bitcast(I32), d_scales[0].bitcast(I32))
+        nc.sync.dma_start(lists["n2"][:], n2)
+        nc.sync.dma_start(dw_win[:], words_of(d_words))
+        nc.sync.dma_start(lists["n3"][:], n3)
+
+        xs = tile("xs", [P, S], U8)
+        xw = tile("xw", [P, S], U32)
+        w1w = tile("w1w", [P, S], U32)
+        w1s = tile("w1s", [P, S], U8)
+        nc.vector.tensor_copy(xs[:], xs_win[:].indirect(lists["offs"][:]))
+        halves = ((0, 256), (256, 512))
+        y_banks = [ps.tile([P, S], F32, name="y_bank%d" % t) for t in range(PACK)]
+        for n, (lo, hi) in enumerate(halves):
+            nc.vector.tensor_copy(xw[:, lo:hi], xw_win[:].bitcast(U32).indirect(entries("offs", lo, hi)))
+            if n == 0:
+                deal(nc.gpsimd, w1s[:], w1s_raw[:], 16)
+                deal(nc.vector, w1w[:], w1w_raw[:].bitcast(U32), 4)
+            for t in range(PACK):
+                cols = slice(t * P, (t + 1) * P)
+                nc.tensor.matmul_mx(
+                    out=y_banks[t][:, lo:hi],
+                    lhsT=w1w[:, cols].bitcast(FP8X4),
+                    lhsT_scale=w1s[:, cols],
+                    rhs=xw[:, lo:hi].bitcast(FP8X4),
+                    rhs_scale=xs[:, lo:hi],
+                    start=True,
+                    stop=True,
+                )
+
+        ds_got = tile("ds_got", [P, S], U8)
+        ds_dealt = tile("ds_dealt", [P, S], U8)
+        nc.vector.tensor_copy(ds_got[:], ds_win[:].indirect(lists["k1"][:]))
+        deal(nc.vector, ds_dealt[:], ds_got[:], 16)
+        for q in range(4):
+            nc.sync.dma_start(ds_plane[32 * q : 32 * q + 4, :].bitcast(I32), ds_dealt[32 * q : 32 * q + 32 : 8, :].bitcast(I32))
+
+        y_win = [tile("y_win%d" % t, [P, S], F32) for t in range(PACK)]
+        gy_win = [tile("gy_win%d" % t, [P, S], F32) for t in range(PACK)]
+        for t in range(PACK):
+            nc.scalar.copy(y_win[t][:], y_banks[t][:])
+            nc.scalar.activation(gy_win[t][:], y_banks[t][:], ACT.Copy, scale=gain[:, t : t + 1])
+
+        dw_got = tile("dw_got", [P, S], U32)
+        dw = tile("dw", [P, S], U32)
+        zw = tile("zw", [P, S], U32)
+        zs = tile("zs", [P, S], U8)
+        h_banks = [ps.tile([P, PACK, CH], F32, name="h_bank%d" % c) for c in range(NCH)]
+        h_win = [tile("h_win%d" % t, [P, S], F32) for t in range(PACK)]
+        h_sq = [tile("h_sq%d" % c, [P, PACK, CH], F32) for c in range(NCH)]
+
+        sixteenth = []
+        for n in range(len(Z_PIECES)):
+            sixteenth.append(tile("sixteenth%d" % n, [P, 1], F32, slot="chain%d" % (n + 1)))
+            nc.vector.memset(sixteenth[n][:], 0.0625)
+        first, zb = {}, {}
+
+        def gather_first(n):
+            lo, hi = Z_PIECES[n]
+            first[n] = tile("first%d" % n, [P, PACK, hi - lo], F32, slot="first")
+            for t in range(PACK):
+                nc.vector.tensor_copy(first[n][:, t, :], y_win[t][:].indirect(entries("n1", lo, hi)))
+
+        def gather_second(n):
+            lo, hi = Z_PIECES[n]
+            z = tile("z%d" % n, [P, PACK, hi - lo], F32, slot="chain%d" % (n - 1))
+            for t in range(PACK):
+                nc.vector.tensor_tensor(z[:, t, :], gy_win[t][:].indirect(entries("n2", lo, hi)), first[n][:, t, :], MULT)
+            zb[n] = tile("zb%d" % n, [P, PACK * (hi - lo)], BF16, slot="chain%d" % n)
+            interleave(nc, zb[n][:], z[:])
+
+        def square_h(c):
+            nc.scalar.activation(h_sq[c][:], h_banks[c][:], ACT.Square, scale=0.0625)
+
+        def multiply_z(n):
+            lo, hi = Z_PIECES[n]
+            nc.vector.quantize_mx(out=zw[:, lo:hi].bitcast(FP8X4), scales=zs[:, lo:hi], in_=zb[n][:])
+            for c in range(lo // CH, hi // CH):
+                cols = slice(c * CH, (c + 1) * CH)
+                for t in range(PACK):
+                    rows = slice(t * P, (t + 1) * P)
+                    nc.tensor.matmul_mx(
+                        out=h_banks[c][:, t, :],
+                        lhsT=dw[:, rows].bitcast(FP8X4),
+                        lhsT_scale=ds_plane[:, rows],
+                        rhs=zw[:, cols].bitcast(FP8X4),
+                        rhs_scale=zs[:, cols],
+                        start=True,
+                        stop=True,
+                    )
+                for t in range(PACK):
+                    nc.scalar.activation(h_win[t][:, cols], h_banks[c][:, t, :], ACT.Copy, scale=sixteenth[n][:])
+
+        gather_first(0)
+        gather_second(0)
+        nc.vector.tensor_copy(dw_got[:], dw_win[:].bitcast(U32).indirect(lists["k1"][:]))
+        deal(nc.vector, dw[:], dw_got[:], 4)
+        gather_first(1)
+        multiply_z(0)
+        square_h(0)
+        gather_second(1)
+        square_h(1)
+        gather_first(2)
+        multiply_z(1)
+        gather_second(2)
+        multiply_z(2)
+
+        ow = tile("ow", [P, S], U32)
+        osc = tile("osc", [P, S], U8)
+        out_rows = out_0.rearrange("(p t) j -> p t j", t=PACK)
+        pa, num, pa_sq, den, root, inv, res, resb = {}, {}, {}, {}, {}, {}, {}, {}
+
+        def fetch(c):
+            pa[c] = tile("pa%d" % c, [P, PACK, CH], F32, slot="sq%d" % (c - 2))
+            pa_sq[c] = tile("pa_sq%d" % c, [P, PACK, CH], F32, slot="sq%d" % c)
+            for t in range(PACK):
+                nc.vector.tensor_copy(pa[c][:, t, :], h_win[t][:].indirect(entries("n3", c * CH, (c + 1) * CH)))
+            nc.scalar.activation(pa_sq[c][:], pa[c][:], ACT.Square)
+            if c >= 2:
+                square_h(c)
+
+        def invert(c):
+            den[c] = tile("den%d" % c, [P, PACK, CH], F32)
+            root[c] = tile("root%d" % c, [P, PACK, CH], F32)
+            inv[c] = tile("inv%d" % c, [P, PACK, CH], F32)
+            nc.vector.scalar_tensor_tensor(den[c][:], pa_sq[c][:], 0.5, h_sq[c][:], ADD, ADD)
+            num[c] = tile("num%d" % c, [P, PACK, CH], F32, slot="h_sq%d" % c)
+            nc.vector.scalar_tensor_tensor(num[c][:], h_banks[c][:], 0.125, pa[c][:], MULT, MULT)
+            nc.scalar.activation(root[c][:], den[c][:], ACT.Abs_reciprocal_sqrt)
+            nc.scalar.activation(inv[c][:], root[c][:], ACT.Square)
+
+        def finish(c):
+            cols = slice(c * CH, (c + 1) * CH)
+            res[c] = tile("res%d" % c, [P, PACK, CH], F32)
+            resb[c] = tile("resb%d" % c, [P, PACK * CH], BF16)
+            nc.vector.tensor_tensor(res[c][:], num[c][:], inv[c][:], MULT)
+            interleave(nc, resb[c][:], res[c][:])
+            nc.sync.dma_start(out_rows[:, :, cols], res[c][:])
+
+        def pack(c):
+            cols = slice(c * CH, (c + 1) * CH)
+            nc.vector.quantize_mx(out=ow[:, cols].bitcast(FP8X4), scales=osc[:, cols], in_=resb[c][:])
+            nc.sync.dma_start(words_of(out_1)[:, cols], ow[:, cols].bitcast(I32))
+
+        stages = (fetch, invert, finish, pack)
+        for step in range(NCH + len(stages) - 1):
+            for k, stage in enumerate(stages):
+                if 0 <= step - k < NCH:
+                    stage(step - k)
+        for q in range(4):
+            nc.scalar.dma_start(out_2[0, 4 * q : 4 * q + 4, :].bitcast(I32), osc[32 * q : 32 * q + 4, :].bitcast(I32))

@@ -1,6 +1,7 @@
 from contextlib import ExitStack
 
 import concourse.mybir as mybir
+from concourse.masks import make_identity
 
 F32 = mybir.dt.float32
 BF16 = mybir.dt.bfloat16
@@ -14,27 +15,34 @@ MULT = mybir.AluOpType.mult
 ADD = mybir.AluOpType.add
 
 P = 128
-PACK = 4
+PARTS = 4
+QUADS = 4
 S = 512
 TABLE = 2048
 CH = 128
 NCH = S // CH
-Z_PIECES = ((0, 256), (256, 384), (384, 512))
+LAST = NCH - 1
+Z_PIECES = (((0, 256), (256, 384)), ((384, 512),))
 FLOPS = 2 * 2 * 512 * 512 * 512
 
 
-def deal(engine, dst, src, run):
-    engine.tensor_copy(
-        out=dst.rearrange("p (t b i) -> p b t i", t=PACK, i=run),
-        in_=src.rearrange("p (b i t) -> p b t i", t=PACK, i=run),
+def deal(nc, dst, src, run):
+    nc.vector.tensor_copy(
+        out=dst.rearrange("p (t b i) -> p b t i", t=PARTS, i=run),
+        in_=src.rearrange("p (b i t) -> p b t i", t=PARTS, i=run),
     )
 
 
-def interleave(nc, dst, src):
-    nc.scalar.copy(
-        out=dst.rearrange("p (c i t) -> p c t i", t=PACK, i=PACK),
-        in_=src.rearrange("p t (c i) -> p c t i", i=PACK),
-    )
+def woven(ap):
+    return ap.rearrange("p (c i t) -> p c t i", t=PARTS, i=2)
+
+
+def walked(ap):
+    return ap.rearrange("p t (c i) -> p c t i", i=2)
+
+
+def words_of(ap):
+    return ap[0].rearrange("p n t -> p (n t)").bitcast(I32)
 
 
 def tile_picked_denseprodharm_none_po_kernel(
@@ -55,183 +63,199 @@ def tile_picked_denseprodharm_none_po_kernel(
         def entries(name, lo, hi):
             return lists[name][:, lo // 16 : hi // 16]
 
-        def words_of(ap):
-            return ap[0].rearrange("p n t -> p (n t)").bitcast(I32)
+        def scale_rows(sbuf, q):
+            return sbuf[32 * q : 32 * q + 4, :].bitcast(I32)
+
+        def scale_source(dram, q):
+            return dram[0, 4 * q : 4 * q + 4, :].bitcast(I32)
 
         xs_win = tile("xs_win", [P, TABLE], U8)
-        w1s_raw = tile("w1s_raw", [P, S], U8)
         ds_win = tile("ds_win", [P, TABLE], U8)
+        w1s_raw = tile("w1s_raw", [P, S], U8)
         ds_plane = tile("ds_plane", [P, S], U8)
-        warm = tile("warm", [P, 2], F32)
-        nc.vector.memset(xs_win[:].bitcast(I32), 0)
-        nc.vector.memset(w1s_raw[:].bitcast(I32), 0)
-        nc.vector.memset(warm[:, 0:1], 1.0)
-        nc.vector.memset(ds_win[:].bitcast(I32), 0)
-        nc.vector.memset(ds_plane[:].bitcast(I32), 0)
+        for zeroed in (xs_win, ds_win, w1s_raw, ds_plane):
+            nc.vector.memset(zeroed[:].bitcast(I32), 0)
+        sixteenth = tile("sixteenth", [P, 1], F32, slot="pa_rest")
+        nc.vector.memset(sixteenth[:], 0.0625)
+        ident = tile("ident", [P, P], F32)
+        nc.vector.memset(ident[:], 0.0)
+        make_identity(nc, ident[:], nomemset=True)
 
         xw_win = tile("xw_win", [P, TABLE], I32)
         w1w_raw = tile("w1w_raw", [P, S], I32)
         dw_win = tile("dw_win", [P, TABLE], I32)
-        gain = tile("gain", [P, PACK], F32)
+        gain = tile("gain", [P, PARTS], F32)
 
         nc.sync.dma_start(lists["offs"][:], offs)
         nc.sync.dma_start(lists["k1"][:], k1)
-        nc.sync.dma_start(lists["n1"][:], n1)
-        nc.sync.dma_start(xw_win[:], words_of(x_words))
-        nc.gpsimd.dma_start(gain[:], gs.rearrange("(p t) o -> p (t o)", t=PACK))
-        for q in range(4):
-            nc.scalar.dma_start(xs_win[32 * q : 32 * q + 4, :].bitcast(I32), x_scales[0, 4 * q : 4 * q + 4, :].bitcast(I32))
-        nc.scalar.activation(warm[:, 1:2], warm[:, 0:1], ACT.Abs_reciprocal_sqrt)
-        nc.sync.dma_start(w1w_raw[:], words_of(w1_words))
-        for q in range(4):
-            nc.scalar.dma_start(w1s_raw[32 * q : 32 * q + 4, :].bitcast(I32), w1_scales[0, 4 * q : 4 * q + 4, :].bitcast(I32))
+        for q in range(QUADS):
+            nc.sync.dma_start(scale_rows(xs_win, q), scale_source(x_scales, q))
         nc.sync.dma_start(ds_win[0:P:8, :].bitcast(I32), d_scales[0].bitcast(I32))
-        nc.sync.dma_start(lists["n2"][:], n2)
+        nc.sync.dma_start(xw_win[:], words_of(x_words))
+        nc.sync.dma_start(w1w_raw[:], words_of(w1_words))
+        for q in range(QUADS):
+            nc.sync.dma_start(scale_rows(w1s_raw, q), scale_source(w1_scales, q))
         nc.sync.dma_start(dw_win[:], words_of(d_words))
+        nc.sync.dma_start(lists["n1"][:], n1)
+        nc.sync.dma_start(lists["n2"][:], n2)
+        nc.sync.dma_start(gain[:], gs.rearrange("(p t) o -> p (t o)", t=PARTS))
         nc.sync.dma_start(lists["n3"][:], n3)
+        warm = tile("warm", [P, 1], F32)
+        nc.scalar.activation(warm[:], sixteenth[:], ACT.Abs_reciprocal_sqrt)
 
         xs = tile("xs", [P, S], U8)
         xw = tile("xw", [P, S], U32)
         w1w = tile("w1w", [P, S], U32)
         w1s = tile("w1s", [P, S], U8)
         nc.vector.tensor_copy(xs[:], xs_win[:].indirect(lists["offs"][:]))
-        halves = ((0, 256), (256, 512))
-        y_banks = [ps.tile([P, S], F32, name="y_bank%d" % t) for t in range(PACK)]
-        for n, (lo, hi) in enumerate(halves):
-            nc.vector.tensor_copy(xw[:, lo:hi], xw_win[:].bitcast(U32).indirect(entries("offs", lo, hi)))
-            if n == 0:
-                deal(nc.gpsimd, w1s[:], w1s_raw[:], 16)
-                deal(nc.vector, w1w[:], w1w_raw[:].bitcast(U32), 4)
-            for t in range(PACK):
-                cols = slice(t * P, (t + 1) * P)
-                nc.tensor.matmul_mx(
-                    out=y_banks[t][:, lo:hi],
-                    lhsT=w1w[:, cols].bitcast(FP8X4),
-                    lhsT_scale=w1s[:, cols],
-                    rhs=xw[:, lo:hi].bitcast(FP8X4),
-                    rhs_scale=xs[:, lo:hi],
-                    start=True,
-                    stop=True,
-                )
-
-        ds_got = tile("ds_got", [P, S], U8)
-        ds_dealt = tile("ds_dealt", [P, S], U8)
+        ds_got = tile("ds_got", [P, S], U8, slot="xs_win")
         nc.vector.tensor_copy(ds_got[:], ds_win[:].indirect(lists["k1"][:]))
-        deal(nc.vector, ds_dealt[:], ds_got[:], 16)
-        for q in range(4):
-            nc.sync.dma_start(ds_plane[32 * q : 32 * q + 4, :].bitcast(I32), ds_dealt[32 * q : 32 * q + 32 : 8, :].bitcast(I32))
+        nc.vector.tensor_copy(xw[:], xw_win[:].bitcast(U32).indirect(lists["offs"][:]))
+        deal(nc, w1w[:], w1w_raw[:].bitcast(U32), 4)
+        deal(nc, w1s[:], w1s_raw[:], 16)
+        y_banks = [ps.tile([P, S], F32, name="y_bank%d" % t, tag="bank%d" % t) for t in range(PARTS)]
+        for t in range(PARTS):
+            rows = slice(t * P, (t + 1) * P)
+            nc.tensor.matmul_mx(
+                out=y_banks[t][:],
+                lhsT=w1w[:, rows].bitcast(FP8X4),
+                lhsT_scale=w1s[:, rows],
+                rhs=xw[:].bitcast(FP8X4),
+                rhs_scale=xs[:],
+                start=True,
+                stop=True,
+            )
 
-        y_win = [tile("y_win%d" % t, [P, S], F32) for t in range(PACK)]
-        gy_win = [tile("gy_win%d" % t, [P, S], F32) for t in range(PACK)]
-        for t in range(PACK):
+        ds_dealt = tile("ds_dealt", [P, S], U8, slot="w1s_raw")
+        deal(nc, ds_dealt[:], ds_got[:], 16)
+        for q in range(QUADS):
+            nc.sync.dma_start(scale_rows(ds_plane, q), ds_dealt[32 * q : 32 * q + 32 : 8, :].bitcast(I32))
+
+        y_win = [tile("y_win%d" % t, [P, S], F32) for t in range(PARTS)]
+        gy_win = [tile("gy_win%d" % t, [P, S], F32) for t in range(PARTS)]
+        for t in range(PARTS):
             nc.scalar.copy(y_win[t][:], y_banks[t][:])
             nc.scalar.activation(gy_win[t][:], y_banks[t][:], ACT.Copy, scale=gain[:, t : t + 1])
 
         dw_got = tile("dw_got", [P, S], U32)
         dw = tile("dw", [P, S], U32)
+        nc.vector.tensor_copy(dw_got[:], dw_win[:].bitcast(U32).indirect(lists["k1"][:]))
+        deal(nc, dw[:], dw_got[:], 4)
+
+        h_parts = []
+        for c in range(NCH):
+            h_parts.append([(ps.tile([P, PARTS, CH], F32, name="h_bank%d" % c), 0, PARTS if c < LAST else PARTS // 2)])
+        h_parts[LAST].append((ps.tile([P, PARTS, CH], F32, name="h_last", tag="bank3"), PARTS // 2, PARTS))
+        h_win = [tile("h_win%d" % t, [P, S], F32) for t in range(PARTS)]
         zw = tile("zw", [P, S], U32)
         zs = tile("zs", [P, S], U8)
-        h_banks = [ps.tile([P, PACK, CH], F32, name="h_bank%d" % c) for c in range(NCH)]
-        h_win = [tile("h_win%d" % t, [P, S], F32) for t in range(PACK)]
-        h_sq = [tile("h_sq%d" % c, [P, PACK, CH], F32) for c in range(NCH)]
+        first = tile("first", [P, PARTS, S - CH], F32)
+        second = tile("second", [P, PARTS, S - CH], F32)
 
-        sixteenth = []
-        for n in range(len(Z_PIECES)):
-            sixteenth.append(tile("sixteenth%d" % n, [P, 1], F32, slot="chain%d" % (n + 1)))
-            nc.vector.memset(sixteenth[n][:], 0.0625)
-        first, zb = {}, {}
+        for n, runs in enumerate(Z_PIECES):
+            lo, hi = runs[0][0], runs[-1][1]
+            for t in range(PARTS):
+                nc.vector.tensor_copy(first[:, t, 0 : hi - lo], y_win[t][:].indirect(entries("n1", lo, hi)))
+                nc.vector.tensor_copy(second[:, t, 0 : hi - lo], gy_win[t][:].indirect(entries("n2", lo, hi)))
+            zb = tile("zb%d" % n, [P, PARTS * (hi - lo)], BF16)
+            for a, b in runs:
+                held = slice(a - lo, b - lo)
+                z_run = zb[:, PARTS * (a - lo) : PARTS * (b - lo)]
+                nc.vector.tensor_tensor(woven(z_run), walked(first[:, :, held]), walked(second[:, :, held]), MULT)
+            for a, b in runs:
+                z_run = zb[:, PARTS * (a - lo) : PARTS * (b - lo)]
+                nc.vector.quantize_mx(out=zw[:, a:b].bitcast(FP8X4), scales=zs[:, a:b], in_=z_run)
+                for c in range(a // CH, b // CH):
+                    cols = slice(c * CH, (c + 1) * CH)
+                    for bank, t_lo, t_hi in h_parts[c]:
+                        for t in range(t_lo, t_hi):
+                            rows = slice(t * P, (t + 1) * P)
+                            nc.tensor.matmul_mx(
+                                out=bank[:, t, :],
+                                lhsT=dw[:, rows].bitcast(FP8X4),
+                                lhsT_scale=ds_plane[:, rows],
+                                rhs=zw[:, cols].bitcast(FP8X4),
+                                rhs_scale=zs[:, cols],
+                                start=True,
+                                stop=True,
+                            )
+                    for bank, t_lo, t_hi in h_parts[c]:
+                        for t in range(t_lo, t_hi):
+                            if t_lo == 0:
+                                nc.scalar.activation(h_win[t][:, cols], bank[:, t, :], ACT.Copy, scale=0.0625)
+                            else:
+                                nc.vector.tensor_scalar(h_win[t][:, cols], bank[:, t, :], 0.0625, None, MULT)
 
-        def gather_first(n):
-            lo, hi = Z_PIECES[n]
-            first[n] = tile("first%d" % n, [P, PACK, hi - lo], F32, slot="first")
-            for t in range(PACK):
-                nc.vector.tensor_copy(first[n][:, t, :], y_win[t][:].indirect(entries("n1", lo, hi)))
+        h_sq = []
+        for c in range(NCH):
+            h_sq.append(tile("h_sq%d" % c, [P, PARTS, CH], F32))
+            for bank, t_lo, t_hi in h_parts[c]:
+                factor = sixteenth[:] if c == 1 else 0.0625
+                nc.scalar.activation(h_sq[c][:, t_lo:t_hi, :], bank[:, t_lo:t_hi, :], ACT.Square, scale=factor)
 
-        def gather_second(n):
-            lo, hi = Z_PIECES[n]
-            z = tile("z%d" % n, [P, PACK, hi - lo], F32, slot="chain%d" % (n - 1))
-            for t in range(PACK):
-                nc.vector.tensor_tensor(z[:, t, :], gy_win[t][:].indirect(entries("n2", lo, hi)), first[n][:, t, :], MULT)
-            zb[n] = tile("zb%d" % n, [P, PACK * (hi - lo)], BF16, slot="chain%d" % n)
-            interleave(nc, zb[n][:], z[:])
+        pa_first = tile("pa_first", [P, PARTS, CH], F32)
+        pa_rest = tile("pa_rest", [P, PARTS, S - CH], F32)
+        pa = [pa_first[:]] + [pa_rest[:, :, c * CH : (c + 1) * CH] for c in range(NCH - 1)]
+        for c in range(NCH):
+            for t in range(PARTS):
+                nc.vector.tensor_copy(pa[c][:, t, :], h_win[t][:].indirect(entries("n3", c * CH, (c + 1) * CH)))
 
-        def square_h(c):
-            nc.scalar.activation(h_sq[c][:], h_banks[c][:], ACT.Square, scale=0.0625)
+        pa_sq, inv = {}, {}
 
-        def multiply_z(n):
-            lo, hi = Z_PIECES[n]
-            nc.vector.quantize_mx(out=zw[:, lo:hi].bitcast(FP8X4), scales=zs[:, lo:hi], in_=zb[n][:])
-            for c in range(lo // CH, hi // CH):
-                cols = slice(c * CH, (c + 1) * CH)
-                for t in range(PACK):
-                    rows = slice(t * P, (t + 1) * P)
-                    nc.tensor.matmul_mx(
-                        out=h_banks[c][:, t, :],
-                        lhsT=dw[:, rows].bitcast(FP8X4),
-                        lhsT_scale=ds_plane[:, rows],
-                        rhs=zw[:, cols].bitcast(FP8X4),
-                        rhs_scale=zs[:, cols],
-                        start=True,
-                        stop=True,
-                    )
-                for t in range(PACK):
-                    nc.scalar.activation(h_win[t][:, cols], h_banks[c][:, t, :], ACT.Copy, scale=sixteenth[n][:])
+        def square_pa(c):
+            pa_sq[c] = tile("pa_sq%d" % c, [P, PARTS, CH], F32, slot="pa_sq%d" % (c % 2))
+            nc.scalar.activation(pa_sq[c][:], pa[c], ACT.Square)
 
-        gather_first(0)
-        gather_second(0)
-        nc.vector.tensor_copy(dw_got[:], dw_win[:].bitcast(U32).indirect(lists["k1"][:]))
-        deal(nc.vector, dw[:], dw_got[:], 4)
-        gather_first(1)
-        multiply_z(0)
-        square_h(0)
-        gather_second(1)
-        square_h(1)
-        gather_first(2)
-        multiply_z(1)
-        gather_second(2)
-        multiply_z(2)
+        def invert(c):
+            root = tile("root%d" % c, [P, PARTS, CH], F32)
+            squared = tile("inv%d" % c, [P, PARTS, CH], F32)
+            if c < LAST:
+                turned = ps.tile([P, PARTS, P], F32, name="turned%d" % c, tag="bank%d" % (c % 2))
+                for t in range(PARTS):
+                    nc.tensor.matmul(turned[:, t, :], h_sq[c][:, t, :], ident[:], start=True, stop=False, is_transpose=True)
+                    nc.tensor.matmul(turned[:, t, :], pa_sq[c][:, t, :], ident[:], start=False, stop=True, is_transpose=True)
+                nc.scalar.activation(root[:], turned[:], ACT.Abs_reciprocal_sqrt, bias=0.5)
+                nc.scalar.activation(squared[:], root[:], ACT.Square)
+                free_bank = "bank2" if c == 0 else "h_bank%d" % (c - 1)
+                inv[c] = ps.tile([P, PARTS, CH], F32, name="inv_back%d" % c, tag=free_bank)
+                for t in range(PARTS):
+                    nc.tensor.transpose(inv[c][:, t, :], squared[:, t, :], ident[:])
+            else:
+                den = tile("den", [P, PARTS, CH], F32)
+                nc.vector.scalar_tensor_tensor(den[:], pa_sq[c][:], 0.5, h_sq[c][:], ADD, ADD)
+                nc.scalar.activation(root[:], den[:], ACT.Abs_reciprocal_sqrt)
+                nc.scalar.activation(squared[:], root[:], ACT.Square)
+                inv[c] = squared
+
+        square_pa(0)
+        square_pa(1)
+        for c in range(NCH):
+            invert(c)
+            if c + 2 < NCH:
+                square_pa(c + 2)
+
+        num = []
+        for c in range(NCH):
+            num.append(tile("num%d" % c, [P, PARTS, CH], F32, slot="h_sq%d" % c))
+            for bank, t_lo, t_hi in h_parts[c]:
+                held = slice(t_lo, t_hi)
+                nc.vector.scalar_tensor_tensor(num[c][:, held, :], bank[:, held, :], 0.125, pa[c][:, held, :], MULT, MULT)
 
         ow = tile("ow", [P, S], U32)
         osc = tile("osc", [P, S], U8)
-        out_rows = out_0.rearrange("(p t) j -> p t j", t=PACK)
-        pa, num, pa_sq, den, root, inv, res, resb = {}, {}, {}, {}, {}, {}, {}, {}
-
-        def fetch(c):
-            pa[c] = tile("pa%d" % c, [P, PACK, CH], F32, slot="sq%d" % (c - 2))
-            pa_sq[c] = tile("pa_sq%d" % c, [P, PACK, CH], F32, slot="sq%d" % c)
-            for t in range(PACK):
-                nc.vector.tensor_copy(pa[c][:, t, :], h_win[t][:].indirect(entries("n3", c * CH, (c + 1) * CH)))
-            nc.scalar.activation(pa_sq[c][:], pa[c][:], ACT.Square)
-            if c >= 2:
-                square_h(c)
-
-        def invert(c):
-            den[c] = tile("den%d" % c, [P, PACK, CH], F32)
-            root[c] = tile("root%d" % c, [P, PACK, CH], F32)
-            inv[c] = tile("inv%d" % c, [P, PACK, CH], F32)
-            nc.vector.scalar_tensor_tensor(den[c][:], pa_sq[c][:], 0.5, h_sq[c][:], ADD, ADD)
-            num[c] = tile("num%d" % c, [P, PACK, CH], F32, slot="h_sq%d" % c)
-            nc.vector.scalar_tensor_tensor(num[c][:], h_banks[c][:], 0.125, pa[c][:], MULT, MULT)
-            nc.scalar.activation(root[c][:], den[c][:], ACT.Abs_reciprocal_sqrt)
-            nc.scalar.activation(inv[c][:], root[c][:], ACT.Square)
-
-        def finish(c):
+        out_rows = out_0.rearrange("(p t) j -> p t j", t=PARTS)
+        for c in range(NCH):
             cols = slice(c * CH, (c + 1) * CH)
-            res[c] = tile("res%d" % c, [P, PACK, CH], F32)
-            resb[c] = tile("resb%d" % c, [P, PACK * CH], BF16)
-            nc.vector.tensor_tensor(res[c][:], num[c][:], inv[c][:], MULT)
-            interleave(nc, resb[c][:], res[c][:])
-            nc.sync.dma_start(out_rows[:, :, cols], res[c][:])
-
-        def pack(c):
-            cols = slice(c * CH, (c + 1) * CH)
-            nc.vector.quantize_mx(out=ow[:, cols].bitcast(FP8X4), scales=osc[:, cols], in_=resb[c][:])
-            nc.sync.dma_start(words_of(out_1)[:, cols], ow[:, cols].bitcast(I32))
-
-        stages = (fetch, invert, finish, pack)
-        for step in range(NCH + len(stages) - 1):
-            for k, stage in enumerate(stages):
-                if 0 <= step - k < NCH:
-                    stage(step - k)
-        for q in range(4):
-            nc.scalar.dma_start(out_2[0, 4 * q : 4 * q + 4, :].bitcast(I32), osc[32 * q : 32 * q + 4, :].bitcast(I32))
+            res = tile("res%d" % c, [P, PARTS, CH], F32)
+            nc.vector.tensor_tensor(res[:], num[c][:], inv[c][:], MULT)
+            nc.sync.dma_start(out_rows[:, :, cols], res[:])
+            resb = tile("resb%d" % c, [P, PARTS * CH], BF16)
+            round_to_bf16 = nc.scalar.copy if c < LAST else nc.vector.tensor_copy
+            round_to_bf16(woven(resb[:]), walked(res[:]))
+            nc.vector.quantize_mx(out=ow[:, cols].bitcast(FP8X4), scales=osc[:, cols], in_=resb[:])
+            if c >= LAST - 1:
+                stored = slice(0, LAST * CH) if c < LAST else cols
+                nc.sync.dma_start(words_of(out_1)[:, stored], ow[:, stored].bitcast(I32))
+        for q in range(QUADS):
+            queue = nc.scalar if q < QUADS - 1 else nc.sync
+            queue.dma_start(scale_source(out_2, q), scale_rows(osc, q))

@@ -22,7 +22,8 @@ TABLE = 2048
 CH = 128
 NCH = S // CH
 LAST = NCH - 1
-Z_PIECES = (((0, 256), (256, 384)), ((384, 512),))
+WIDE = S - CH
+WIDE_RUNS = ((0, 256), (256, WIDE))
 FLOPS = 2 * 2 * 512 * 512 * 512
 
 
@@ -149,42 +150,50 @@ def tile_picked_denseprodharm_none_po_kernel(
         h_win = [tile("h_win%d" % t, [P, S], F32) for t in range(PARTS)]
         zw = tile("zw", [P, S], U32)
         zs = tile("zs", [P, S], U8)
-        first = tile("first", [P, PARTS, S - CH], F32)
-        second = tile("second", [P, PARTS, S - CH], F32)
 
-        for n, runs in enumerate(Z_PIECES):
-            lo, hi = runs[0][0], runs[-1][1]
-            for t in range(PARTS):
-                nc.vector.tensor_copy(first[:, t, 0 : hi - lo], y_win[t][:].indirect(entries("n1", lo, hi)))
-                nc.vector.tensor_copy(second[:, t, 0 : hi - lo], gy_win[t][:].indirect(entries("n2", lo, hi)))
-            zb = tile("zb%d" % n, [P, PARTS * (hi - lo)], BF16)
-            for a, b in runs:
-                held = slice(a - lo, b - lo)
-                z_run = zb[:, PARTS * (a - lo) : PARTS * (b - lo)]
-                nc.vector.tensor_tensor(woven(z_run), walked(first[:, :, held]), walked(second[:, :, held]), MULT)
-            for a, b in runs:
-                z_run = zb[:, PARTS * (a - lo) : PARTS * (b - lo)]
-                nc.vector.quantize_mx(out=zw[:, a:b].bitcast(FP8X4), scales=zs[:, a:b], in_=z_run)
-                for c in range(a // CH, b // CH):
-                    cols = slice(c * CH, (c + 1) * CH)
-                    for bank, t_lo, t_hi in h_parts[c]:
-                        for t in range(t_lo, t_hi):
-                            rows = slice(t * P, (t + 1) * P)
-                            nc.tensor.matmul_mx(
-                                out=bank[:, t, :],
-                                lhsT=dw[:, rows].bitcast(FP8X4),
-                                lhsT_scale=ds_plane[:, rows],
-                                rhs=zw[:, cols].bitcast(FP8X4),
-                                rhs_scale=zs[:, cols],
-                                start=True,
-                                stop=True,
-                            )
-                    for bank, t_lo, t_hi in h_parts[c]:
-                        for t in range(t_lo, t_hi):
-                            if t_lo == 0:
-                                nc.scalar.activation(h_win[t][:, cols], bank[:, t, :], ACT.Copy, scale=0.0625)
-                            else:
-                                nc.vector.tensor_scalar(h_win[t][:, cols], bank[:, t, :], 0.0625, None, MULT)
+        def multiply(zb, lo, hi):
+            nc.vector.quantize_mx(out=zw[:, lo:hi].bitcast(FP8X4), scales=zs[:, lo:hi], in_=zb[:])
+            for c in range(lo // CH, hi // CH):
+                cols = slice(c * CH, (c + 1) * CH)
+                for bank, t_lo, t_hi in h_parts[c]:
+                    for t in range(t_lo, t_hi):
+                        rows = slice(t * P, (t + 1) * P)
+                        nc.tensor.matmul_mx(
+                            out=bank[:, t, :],
+                            lhsT=dw[:, rows].bitcast(FP8X4),
+                            lhsT_scale=ds_plane[:, rows],
+                            rhs=zw[:, cols].bitcast(FP8X4),
+                            rhs_scale=zs[:, cols],
+                            start=True,
+                            stop=True,
+                        )
+                for bank, t_lo, t_hi in h_parts[c]:
+                    for t in range(t_lo, t_hi):
+                        if t_lo == 0:
+                            nc.scalar.activation(h_win[t][:, cols], bank[:, t, :], ACT.Copy, scale=0.0625)
+                        else:
+                            nc.vector.tensor_scalar(h_win[t][:, cols], bank[:, t, :], 0.0625, None, MULT)
+
+        first = tile("first", [P, PARTS, WIDE], F32)
+        z_wide = tile("z_wide", [P, PARTS, WIDE], F32)
+        for t in range(PARTS):
+            nc.vector.tensor_copy(first[:, t, :], y_win[t][:].indirect(entries("n1", 0, WIDE)))
+        for t in range(PARTS):
+            nc.vector.tensor_tensor(z_wide[:, t, :], gy_win[t][:].indirect(entries("n2", 0, WIDE)), first[:, t, :], MULT)
+        for lo, hi in WIDE_RUNS:
+            zb = tile("zb%d" % lo, [P, PARTS * (hi - lo)], BF16, slot="zb%d" % hi)
+            nc.scalar.copy(woven(zb[:]), walked(z_wide[:, :, lo:hi]))
+            multiply(zb, lo, hi)
+
+        first = tile("first_narrow", [P, PARTS, CH], F32, slot="first")
+        second = tile("second_narrow", [P, PARTS, CH], F32, slot="zb%d" % WIDE)
+        for t in range(PARTS):
+            nc.vector.tensor_copy(first[:, t, :], y_win[t][:].indirect(entries("n1", WIDE, S)))
+        for t in range(PARTS):
+            nc.vector.tensor_copy(second[:, t, :], gy_win[t][:].indirect(entries("n2", WIDE, S)))
+        zb = tile("zb_narrow", [P, PARTS * CH], BF16)
+        nc.vector.tensor_tensor(woven(zb[:]), walked(first[:]), walked(second[:]), MULT)
+        multiply(zb, WIDE, S)
 
         h_sq = []
         for c in range(NCH):
@@ -212,8 +221,10 @@ def tile_picked_denseprodharm_none_po_kernel(
             if c < LAST:
                 turned = ps.tile([P, PARTS, P], F32, name="turned%d" % c, tag="bank%d" % (c % 2))
                 for t in range(PARTS):
-                    nc.tensor.matmul(turned[:, t, :], h_sq[c][:, t, :], ident[:], start=True, stop=False, is_transpose=True)
-                    nc.tensor.matmul(turned[:, t, :], pa_sq[c][:, t, :], ident[:], start=False, stop=True, is_transpose=True)
+                    nc.tensor.matmul(turned[:, t, :], h_sq[c][:, t, :], ident[:], start=t == 0, stop=False, is_transpose=True)
+                for t in range(PARTS):
+                    closes = t == PARTS - 1
+                    nc.tensor.matmul(turned[:, t, :], pa_sq[c][:, t, :], ident[:], start=False, stop=closes, is_transpose=True)
                 nc.scalar.activation(root[:], turned[:], ACT.Abs_reciprocal_sqrt, bias=0.5)
                 nc.scalar.activation(squared[:], root[:], ACT.Square)
                 free_bank = "bank2" if c == 0 else "h_bank%d" % (c - 1)
@@ -236,7 +247,7 @@ def tile_picked_denseprodharm_none_po_kernel(
 
         num = []
         for c in range(NCH):
-            num.append(tile("num%d" % c, [P, PARTS, CH], F32, slot="h_sq%d" % c))
+            num.append(tile("num%d" % c, [P, PARTS, CH], F32, slot=("root%d" if c < 2 else "h_sq%d") % c))
             for bank, t_lo, t_hi in h_parts[c]:
                 held = slice(t_lo, t_hi)
                 nc.vector.scalar_tensor_tensor(num[c][:, held, :], bank[:, held, :], 0.125, pa[c][:, held, :], MULT, MULT)
@@ -250,8 +261,7 @@ def tile_picked_denseprodharm_none_po_kernel(
             nc.vector.tensor_tensor(res[:], num[c][:], inv[c][:], MULT)
             nc.sync.dma_start(out_rows[:, :, cols], res[:])
             resb = tile("resb%d" % c, [P, PARTS * CH], BF16)
-            round_to_bf16 = nc.scalar.copy if c < LAST else nc.vector.tensor_copy
-            round_to_bf16(woven(resb[:]), walked(res[:]))
+            nc.scalar.copy(woven(resb[:]), walked(res[:]))
             nc.vector.quantize_mx(out=ow[:, cols].bitcast(FP8X4), scales=osc[:, cols], in_=resb[:])
             if c >= LAST - 1:
                 stored = slice(0, LAST * CH) if c < LAST else cols

from contextlib import ExitStack

import concourse.mybir as mybir
from concourse.masks import make_identity

F32 = mybir.dt.float32
BF16 = mybir.dt.bfloat16
I32 = mybir.dt.int32
U32 = mybir.dt.uint32
U16 = mybir.dt.uint16
U8 = mybir.dt.uint8
FP8X4 = mybir.dt.float8_e4m3fn_x4
ACT = mybir.ActivationFunctionType
MULT = mybir.AluOpType.mult
ADD = mybir.AluOpType.add

P = 128
PARTS = 4
QUADS = 4
S = 512
TABLE = 2048
CH = 128
NCH = S // CH
LAST = NCH - 1
WIDE = S - CH
WIDE_RUNS = ((0, 256), (256, WIDE))
FLOPS = 2 * 2 * 512 * 512 * 512


def deal(nc, dst, src, run):
    nc.vector.tensor_copy(
        out=dst.rearrange("p (t b i) -> p b t i", t=PARTS, i=run),
        in_=src.rearrange("p (b i t) -> p b t i", t=PARTS, i=run),
    )


def woven(ap):
    return ap.rearrange("p (c i t) -> p c t i", t=PARTS, i=2)


def walked(ap):
    return ap.rearrange("p t (c i) -> p c t i", i=2)


def words_of(ap):
    return ap[0].rearrange("p n t -> p (n t)").bitcast(I32)


def tile_picked_denseprodharm_none_po_kernel(
    tc, x_words, x_scales, w1_words, w1_scales, gs, d_words, d_scales, offs, n1, n2, k1, n3, out_0, out_1, out_2
):
    nc = tc.nc
    with ExitStack() as ctx:
        sb = ctx.enter_context(tc.tile_pool(name="sb", bufs=1))
        ps = ctx.enter_context(tc.psum_pool(name="ps", bufs=1))

        def tile(name, shape, dtype, slot=None):
            return sb.tile(shape, dtype, name=name, tag=slot or name, align_bytes=64)

        lists = {}
        for name in ("offs", "n1", "n2", "k1", "n3"):
            lists[name] = tile("list_" + name, [P, S // 16], U16)

        def entries(name, lo, hi):
            return lists[name][:, lo // 16 : hi // 16]

        def scale_rows(sbuf, q):
            return sbuf[32 * q : 32 * q + 4, :].bitcast(I32)

        def scale_source(dram, q):
            return dram[0, 4 * q : 4 * q + 4, :].bitcast(I32)

        xs_win = tile("xs_win", [P, TABLE], U8)
        ds_win = tile("ds_win", [P, TABLE], U8)
        w1s_raw = tile("w1s_raw", [P, S], U8)
        ds_plane = tile("ds_plane", [P, S], U8)
        for zeroed in (xs_win, ds_win, w1s_raw, ds_plane):
            nc.vector.memset(zeroed[:].bitcast(I32), 0)
        sixteenth = tile("sixteenth", [P, 1], F32, slot="pa_rest")
        nc.vector.memset(sixteenth[:], 0.0625)
        ident = tile("ident", [P, P], F32)
        nc.vector.memset(ident[:], 0.0)
        make_identity(nc, ident[:], nomemset=True)

        xw_win = tile("xw_win", [P, TABLE], I32)
        w1w_raw = tile("w1w_raw", [P, S], I32)
        dw_win = tile("dw_win", [P, TABLE], I32)
        gain = tile("gain", [P, PARTS], F32)

        nc.sync.dma_start(lists["offs"][:], offs)
        nc.sync.dma_start(lists["k1"][:], k1)
        for q in range(QUADS):
            nc.sync.dma_start(scale_rows(xs_win, q), scale_source(x_scales, q))
        nc.sync.dma_start(ds_win[0:P:8, :].bitcast(I32), d_scales[0].bitcast(I32))
        nc.sync.dma_start(xw_win[:], words_of(x_words))
        nc.sync.dma_start(w1w_raw[:], words_of(w1_words))
        for q in range(QUADS):
            nc.sync.dma_start(scale_rows(w1s_raw, q), scale_source(w1_scales, q))
        nc.sync.dma_start(dw_win[:], words_of(d_words))
        nc.sync.dma_start(lists["n1"][:], n1)
        nc.sync.dma_start(lists["n2"][:], n2)
        nc.sync.dma_start(gain[:], gs.rearrange("(p t) o -> p (t o)", t=PARTS))
        nc.sync.dma_start(lists["n3"][:], n3)
        warm = tile("warm", [P, 1], F32)
        nc.scalar.activation(warm[:], sixteenth[:], ACT.Abs_reciprocal_sqrt)

        xs = tile("xs", [P, S], U8)
        xw = tile("xw", [P, S], U32)
        w1w = tile("w1w", [P, S], U32)
        w1s = tile("w1s", [P, S], U8)
        nc.vector.tensor_copy(xs[:], xs_win[:].indirect(lists["offs"][:]))
        ds_got = tile("ds_got", [P, S], U8, slot="xs_win")
        nc.vector.tensor_copy(ds_got[:], ds_win[:].indirect(lists["k1"][:]))
        nc.vector.tensor_copy(xw[:], xw_win[:].bitcast(U32).indirect(lists["offs"][:]))
        deal(nc, w1w[:], w1w_raw[:].bitcast(U32), 4)
        deal(nc, w1s[:], w1s_raw[:], 16)
        y_banks = [ps.tile([P, S], F32, name="y_bank%d" % t, tag="bank%d" % t) for t in range(PARTS)]
        for t in range(PARTS):
            rows = slice(t * P, (t + 1) * P)
            nc.tensor.matmul_mx(
                out=y_banks[t][:],
                lhsT=w1w[:, rows].bitcast(FP8X4),
                lhsT_scale=w1s[:, rows],
                rhs=xw[:].bitcast(FP8X4),
                rhs_scale=xs[:],
                start=True,
                stop=True,
            )

        ds_dealt = tile("ds_dealt", [P, S], U8, slot="w1s_raw")
        deal(nc, ds_dealt[:], ds_got[:], 16)
        for q in range(QUADS):
            nc.sync.dma_start(scale_rows(ds_plane, q), ds_dealt[32 * q : 32 * q + 32 : 8, :].bitcast(I32))

        y_win = [tile("y_win%d" % t, [P, S], F32) for t in range(PARTS)]
        gy_win = [tile("gy_win%d" % t, [P, S], F32) for t in range(PARTS)]
        for t in range(PARTS):
            nc.scalar.copy(y_win[t][:], y_banks[t][:])
            nc.scalar.activation(gy_win[t][:], y_banks[t][:], ACT.Copy, scale=gain[:, t : t + 1])

        dw_got = tile("dw_got", [P, S], U32)
        dw = tile("dw", [P, S], U32)
        nc.vector.tensor_copy(dw_got[:], dw_win[:].bitcast(U32).indirect(lists["k1"][:]))
        deal(nc, dw[:], dw_got[:], 4)

        h_parts = []
        for c in range(NCH):
            h_parts.append([(ps.tile([P, PARTS, CH], F32, name="h_bank%d" % c), 0, PARTS if c < LAST else PARTS // 2)])
        h_parts[LAST].append((ps.tile([P, PARTS, CH], F32, name="h_last", tag="bank3"), PARTS // 2, PARTS))
        h_win = [tile("h_win%d" % t, [P, S], F32) for t in range(PARTS)]
        zw = tile("zw", [P, S], U32)
        zs = tile("zs", [P, S], U8)

        def multiply(zb, lo, hi):
            nc.vector.quantize_mx(out=zw[:, lo:hi].bitcast(FP8X4), scales=zs[:, lo:hi], in_=zb[:])
            for c in range(lo // CH, hi // CH):
                cols = slice(c * CH, (c + 1) * CH)
                for bank, t_lo, t_hi in h_parts[c]:
                    for t in range(t_lo, t_hi):
                        rows = slice(t * P, (t + 1) * P)
                        nc.tensor.matmul_mx(
                            out=bank[:, t, :],
                            lhsT=dw[:, rows].bitcast(FP8X4),
                            lhsT_scale=ds_plane[:, rows],
                            rhs=zw[:, cols].bitcast(FP8X4),
                            rhs_scale=zs[:, cols],
                            start=True,
                            stop=True,
                        )
                for bank, t_lo, t_hi in h_parts[c]:
                    for t in range(t_lo, t_hi):
                        if t_lo == 0:
                            nc.scalar.activation(h_win[t][:, cols], bank[:, t, :], ACT.Copy, scale=0.0625)
                        else:
                            nc.vector.tensor_scalar(h_win[t][:, cols], bank[:, t, :], 0.0625, None, MULT)

        first = tile("first", [P, PARTS, WIDE], F32)
        z_wide = tile("z_wide", [P, PARTS, WIDE], F32)
        for t in range(PARTS):
            nc.vector.tensor_copy(first[:, t, :], y_win[t][:].indirect(entries("n1", 0, WIDE)))
        for t in range(PARTS):
            nc.vector.tensor_tensor(z_wide[:, t, :], gy_win[t][:].indirect(entries("n2", 0, WIDE)), first[:, t, :], MULT)
        for lo, hi in WIDE_RUNS:
            zb = tile("zb%d" % lo, [P, PARTS * (hi - lo)], BF16, slot="zb%d" % hi)
            nc.scalar.copy(woven(zb[:]), walked(z_wide[:, :, lo:hi]))
            multiply(zb, lo, hi)

        first = tile("first_narrow", [P, PARTS, CH], F32, slot="first")
        second = tile("second_narrow", [P, PARTS, CH], F32, slot="zb%d" % WIDE)
        for t in range(PARTS):
            nc.vector.tensor_copy(first[:, t, :], y_win[t][:].indirect(entries("n1", WIDE, S)))
        for t in range(PARTS):
            nc.vector.tensor_copy(second[:, t, :], gy_win[t][:].indirect(entries("n2", WIDE, S)))
        zb = tile("zb_narrow", [P, PARTS * CH], BF16)
        nc.vector.tensor_tensor(woven(zb[:]), walked(first[:]), walked(second[:]), MULT)
        multiply(zb, WIDE, S)

        h_sq = []
        for c in range(NCH):
            h_sq.append(tile("h_sq%d" % c, [P, PARTS, CH], F32))
            for bank, t_lo, t_hi in h_parts[c]:
                factor = sixteenth[:] if c == 1 else 0.0625
                nc.scalar.activation(h_sq[c][:, t_lo:t_hi, :], bank[:, t_lo:t_hi, :], ACT.Square, scale=factor)

        pa_first = tile("pa_first", [P, PARTS, CH], F32)
        pa_rest = tile("pa_rest", [P, PARTS, S - CH], F32)
        pa = [pa_first[:]] + [pa_rest[:, :, c * CH : (c + 1) * CH] for c in range(NCH - 1)]
        for c in range(NCH):
            for t in range(PARTS):
                nc.vector.tensor_copy(pa[c][:, t, :], h_win[t][:].indirect(entries("n3", c * CH, (c + 1) * CH)))

        pa_sq, inv = {}, {}

        def square_pa(c):
            pa_sq[c] = tile("pa_sq%d" % c, [P, PARTS, CH], F32, slot="pa_sq%d" % (c % 2))
            nc.scalar.activation(pa_sq[c][:], pa[c], ACT.Square)

        def invert(c):
            root = tile("root%d" % c, [P, PARTS, CH], F32)
            squared = tile("inv%d" % c, [P, PARTS, CH], F32)
            if c < LAST:
                turned = ps.tile([P, PARTS, P], F32, name="turned%d" % c, tag="bank%d" % (c % 2))
                for t in range(PARTS):
                    nc.tensor.matmul(turned[:, t, :], h_sq[c][:, t, :], ident[:], start=t == 0, stop=False, is_transpose=True)
                for t in range(PARTS):
                    closes = t == PARTS - 1
                    nc.tensor.matmul(turned[:, t, :], pa_sq[c][:, t, :], ident[:], start=False, stop=closes, is_transpose=True)
                nc.scalar.activation(root[:], turned[:], ACT.Abs_reciprocal_sqrt, bias=0.5)
                nc.scalar.activation(squared[:], root[:], ACT.Square)
                free_bank = "bank2" if c == 0 else "h_bank%d" % (c - 1)
                inv[c] = ps.tile([P, PARTS, CH], F32, name="inv_back%d" % c, tag=free_bank)
                for t in range(PARTS):
                    nc.tensor.transpose(inv[c][:, t, :], squared[:, t, :], ident[:])
            else:
                den = tile("den", [P, PARTS, CH], F32)
                nc.vector.scalar_tensor_tensor(den[:], pa_sq[c][:], 0.5, h_sq[c][:], ADD, ADD)
                nc.scalar.activation(root[:], den[:], ACT.Abs_reciprocal_sqrt)
                nc.scalar.activation(squared[:], root[:], ACT.Square)
                inv[c] = squared

        square_pa(0)
        square_pa(1)
        for c in range(NCH):
            invert(c)
            if c + 2 < NCH:
                square_pa(c + 2)

        num = []
        for c in range(NCH):
            num.append(tile("num%d" % c, [P, PARTS, CH], F32, slot=("root%d" if c < 2 else "h_sq%d") % c))
            for bank, t_lo, t_hi in h_parts[c]:
                held = slice(t_lo, t_hi)
                nc.vector.scalar_tensor_tensor(num[c][:, held, :], bank[:, held, :], 0.125, pa[c][:, held, :], MULT, MULT)

        ow = tile("ow", [P, S], U32)
        osc = tile("osc", [P, S], U8)
        out_rows = out_0.rearrange("(p t) j -> p t j", t=PARTS)
        for c in range(NCH):
            cols = slice(c * CH, (c + 1) * CH)
            res = tile("res%d" % c, [P, PARTS, CH], F32)
            nc.vector.tensor_tensor(res[:], num[c][:], inv[c][:], MULT)
            nc.sync.dma_start(out_rows[:, :, cols], res[:])
            resb = tile("resb%d" % c, [P, PARTS * CH], BF16)
            nc.scalar.copy(woven(resb[:]), walked(res[:]))
            nc.vector.quantize_mx(out=ow[:, cols].bitcast(FP8X4), scales=osc[:, cols], in_=resb[:])
            if c >= LAST - 1:
                stored = slice(0, LAST * CH) if c < LAST else cols
                nc.sync.dma_start(words_of(out_1)[:, stored], ow[:, stored].bitcast(I32))
        for q in range(QUADS):
            queue = nc.scalar if q < QUADS - 1 else nc.sync
            queue.dma_start(scale_source(out_2, q), scale_rows(osc, q))
